import numpy as np
import ml_dtypes


def mxq(x, axis, fmt="e4m3"):
    dtype, down = {"e4m3": (ml_dtypes.float8_e4m3fn, 7), "e5m2": (ml_dtypes.float8_e5m2, 14)}[fmt]
    v = np.moveaxis(np.asarray(x, np.float32).astype(ml_dtypes.bfloat16).astype(np.float64), axis, -1)
    blocks = v.reshape(v.shape[:-1] + (-1, 32))
    amax = np.abs(blocks).max(-1, keepdims=True)
    byte = np.maximum(np.where(amax > 0, np.frexp(amax)[1] - 1 + 127, 0) - down, 1)
    scale = np.exp2(byte - 127.0)
    codes = (blocks / scale).astype(np.float32).astype(dtype).astype(np.float64)
    return np.moveaxis((codes * scale).reshape(v.shape), -1, axis)


WIDE = False


def mx_kscale(k):
    if not WIDE:
        return np.ones(k)
    levels = np.array([10, -10, 5, -5, 0])
    if k % 512:
        return np.exp2(np.random.permutation(np.resize(levels, k // 32))).repeat(32)
    a = np.empty((k // 512, 16))
    for p in range(k // 512):
        a[p, :8] = np.random.permutation(np.resize(levels, 8))
        for g in range(8):
            far = levels[np.abs(levels - a[p, g]) >= 10]
            a[p, g + 8] = far[np.random.randint(len(far))]
    return np.exp2(a.ravel()).repeat(32)


def f64(x):
    return np.asarray(x).astype(np.float64)


def striped(idx):
    return np.tile(np.asarray(idx).reshape(-1, 16).T, (8, 1)).astype(np.uint16)


def unstriped(offs):
    return offs[:16].T.reshape(-1).astype(np.int64)


E2M1 = np.array([0.0, 0.5, 1.0, 1.5, 2.0, 3.0, 4.0, 6.0, -0.0, -0.5, -1.0, -1.5, -2.0, -3.0, -4.0, -6.0])


def pack_weight(w, fmt):
    k, n = w.shape
    w = f64(np.asarray(w, np.float32).astype(ml_dtypes.bfloat16)).reshape(k // 32, 32, n)
    amax = np.abs(w).max(1)
    if fmt == "e4m3":
        byte = np.frexp(amax)[1] - 1 + 127 - 7
    else:
        mant, ex = np.frexp(amax / 6.0)
        byte = np.where(mant > 0.5, ex, ex - 1) + 127
    byte = np.clip(np.where(amax > 0, byte, 1), 1, 254)
    scaled = (w * np.exp2(127.0 - byte)[:, None, :]).reshape(k, n).astype(np.float32)
    by_word = np.ascontiguousarray(scaled.reshape(k // 512, 128, 4, n).transpose(0, 1, 3, 2))
    if fmt == "e4m3":
        words = by_word.astype(ml_dtypes.float8_e4m3fn).view(np.uint8)
    else:
        c = by_word.astype(ml_dtypes.float4_e2m1fn).view(np.uint8) & 0xF
        words = (c[..., 0::2] | (c[..., 1::2] << 4)).reshape(k // 512, 128, 2 * n)
    return np.ascontiguousarray(words), np.ascontiguousarray(byte.astype(np.uint8).reshape(k // 512, 16, n))


def unpack_weight(words, scales, fmt):
    g, _, n = scales.shape
    words = np.ascontiguousarray(words).reshape(g, 128, n, -1)
    if fmt == "e4m3":
        vals = words.view(ml_dtypes.float8_e4m3fn).astype(np.float64)
    else:
        nib = np.empty((g, 128, n, 4), np.uint8)
        nib[..., 0::2] = words & 0xF
        nib[..., 1::2] = words >> 4
        vals = E2M1[nib]
    vals = vals * np.repeat(np.exp2(scales.astype(np.float64) - 127.0), 8, axis=1)[..., None]
    return vals.transpose(0, 1, 3, 2).reshape(g * 512, n)


D, T, I, J, U, Z, M = 512, 2048, 512, 512, 1024, 1024, 1024


def setup_inputs():
    n = np.random.standard_normal
    idx = np.random.permutation(T)[:I]
    idx2 = np.random.permutation(U)[:J]
    idx3 = np.random.permutation(Z)[:J]
    idx4 = np.random.permutation(M)[:J]
    fd = mx_kscale(D)
    keysp = pack_weight(n((D, T)) / fd[:, None], "e4m3")
    return {
        "keys_words": keysp[0],
        "keys_scales": keysp[1],
        "notes": (n((D, U)) * 1.0 / np.sqrt(D) * fd[:, None]).astype(np.float32),
        "given": (np.random.uniform(0.3, 1.7, (I, Z))).astype(np.float32),
        "old": (1.0 * n((I, M))).astype(np.float32),
        "fade": (np.random.uniform(0.3, 0.9, (I, 1))).astype(np.float32),
        "offs": striped(idx),
        "offs2": striped(idx2),
        "offs3": striped(idx3),
        "offs4": striped(idx4),
    }


def reference(keys_words, keys_scales, notes, given, old, fade, offs, offs2, offs3, offs4):
    idx = unstriped(offs)
    idx2 = unstriped(offs2)
    idx3 = unstriped(offs3)
    idx4 = unstriped(offs4)
    keysu = unpack_weight(keys_words, keys_scales, "e4m3")
    keysidxg = keysu[:, idx]
    notesidx2q = mxq(f64(notes)[:, idx2], 0, "e4m3")
    g1 = keysidxg.T @ notesidx2q
    g0 = g1 * f64(given)[:, idx3]
    gf = np.zeros((I, M))
    gf[:, idx4] = g0
    y = f64(old) * f64(fade) + gf
    return y

@@ -1,0 +1,152 @@
+from contextlib import ExitStack
+
+import concourse.mybir as mybir
+from concourse.masks import make_identity
+
+F32 = mybir.dt.float32
+BF16 = mybir.dt.bfloat16
+I32 = mybir.dt.int32
+U32 = mybir.dt.uint32
+U16 = mybir.dt.uint16
+U8 = mybir.dt.uint8
+FP8X4 = mybir.dt.float8_e4m3fn_x4
+MULT = mybir.AluOpType.mult
+ADD = mybir.AluOpType.add
+COPY = mybir.ActivationFunctionType.Copy
+
+P = 128
+PACK = 4
+D, T, I, J, U, Z, M = 512, 2048, 512, 512, 1024, 1024, 1024
+TILES = I // P
+HALF = J // 2
+SHARE = 320
+FLOPS = 2 * D * I * J
+
+
+def tile_attend_tab_timestable_keep_kernel(
+    tc, keys_words, keys_scales, notes, given, old, fade, offs, offs2, offs3, offs4, out
+):
+    nc = tc.nc
+
+    def entries(listed, first, last):
+        return listed[:, first // 16 : last // 16]
+
+    with ExitStack() as ctx:
+        lists = ctx.enter_context(tc.tile_pool(name="lists", bufs=1))
+        keep = ctx.enter_context(tc.tile_pool(name="keep", bufs=1))
+        psum = ctx.enter_context(tc.psum_pool(name="psum", bufs=1))
+
+        key_list = lists.tile([P, I // 16], U16, name="key_list")
+        note_list = lists.tile([P, J // 16], U16, name="note_list")
+        given_list = lists.tile([P, J // 16], U16, name="given_list")
+        place_list = lists.tile([P, J // 16], U16, name="place_list")
+
+        pool_words = keep.tile([P, T], I32, name="pool_words", align_bytes=64)
+        pool_scales = keep.tile([P, T], U8, name="pool_scales", align_bytes=64)
+        note_rows = [keep.tile([P, U], F32, name="note_rows%d" % t) for t in range(PACK)]
+        given_rows = [keep.tile([P, Z], F32, name="given_rows%d" % r) for r in range(TILES)]
+        old_rows = [keep.tile([P, M], F32, name="old_rows%d" % r) for r in range(TILES)]
+        placed = [keep.tile([P, M], F32, name="placed%d" % r) for r in range(TILES)]
+        result = [keep.tile([P, M], F32, name="result%d" % r) for r in range(TILES)]
+        fade_rows = keep.tile([P, P], F32, name="fade_rows")
+        identity = keep.tile([P, P], F32, name="identity")
+        fade_cols = keep.tile([P, TILES], F32, name="fade_cols")
+
+        nc.gpsimd.memset(fade_rows[:], 0.0)
+        nc.gpsimd.memset(pool_scales[:].bitcast(I32), 0)
+        make_identity(nc, identity[:])
+        for r in range(TILES):
+            (nc.vector if r < 2 else nc.gpsimd).memset(placed[r][:], 0.0)
+
+        notes_by_place = notes.rearrange("(p t) u -> t p u", t=PACK)
+        scale_rows = keys_scales[0].bitcast(I32)
+        nc.sync.dma_start(note_list[:], offs2)
+        nc.sync.dma_start(fade_rows[0:TILES, :], fade.rearrange("(r p) o -> r (p o)", p=P))
+        nc.sync.dma_start(note_rows[0][:], notes_by_place[0])
+        nc.sync.dma_start(note_rows[1][:], notes_by_place[1])
+        for f in range(4):
+            nc.sync.dma_start(pool_scales[f:P:32, :].bitcast(I32), scale_rows[f:16:4, :])
+        nc.sync.dma_start(note_rows[2][:], notes_by_place[2])
+        nc.sync.dma_start(note_rows[3][:], notes_by_place[3])
+        nc.sync.dma_start(key_list[:], offs)
+        nc.sync.dma_start(pool_words[:], keys_words[0].rearrange("p n t -> p (n t)").bitcast(I32))
+        nc.sync.dma_start(given_list[:], offs3)
+        for r in range(TILES):
+            nc.sync.dma_start(given_rows[r][:], given[r * P : (r + 1) * P, :])
+        nc.sync.dma_start(place_list[:], offs4)
+        for r in range(TILES):
+            nc.sync.dma_start(old_rows[r][:], old[r * P : (r + 1) * P, :])
+
+        turned = psum.tile([P, P], F32, name="turned")
+        nc.tensor.transpose(turned[:], fade_rows[:], identity[:])
+        nc.scalar.activation(fade_cols[:], turned[:, 0:TILES], COPY)
+
+        picked = keep.tile([P, PACK, J], BF16, name="picked")
+        woven = keep.tile([P, J, PACK], BF16, name="woven", align_bytes=64)
+        note_words = keep.tile([P, J], U32, name="note_words", align_bytes=64)
+        note_scales = keep.tile([P, J], U8, name="note_scales", align_bytes=64)
+        key_words = keep.tile([P, I], U32, name="key_words", align_bytes=64)
+        key_scales = keep.tile([P, I], U8, name="key_scales", align_bytes=64)
+
+        for t in range(PACK - 1):
+            nc.scalar.activation(picked[:, t, :], note_rows[t][:].indirect(note_list[:]), COPY)
+        nc.vector.tensor_copy(key_scales[:], pool_scales[:].indirect(key_list[:]))
+        nc.vector.tensor_copy(picked[:, 3, 0:HALF], note_rows[3][:].indirect(entries(note_list, 0, HALF)))
+        nc.scalar.activation(picked[:, 3, HALF:J], note_rows[3][:].indirect(entries(note_list, HALF, J)), COPY)
+        nc.vector.tensor_copy(woven[:], picked[:].rearrange("p t j -> p j t"))
+        nc.vector.tensor_copy(key_words[:], pool_words[:].bitcast(U32).indirect(key_list[:]))
+        nc.vector.quantize_mx(
+            out=note_words[:].bitcast(FP8X4),
+            scales=note_scales[:],
+            in_=woven[:].rearrange("p j t -> p (j t)"),
+        )
+
+        sums = [psum.tile([P, J], F32, name="sums%d" % r) for r in range(TILES)]
+        for r in range(TILES):
+            rows = slice(r * P, (r + 1) * P)
+            nc.tensor.matmul_mx(
+                out=sums[r][:],
+                lhsT=key_words[:, rows].bitcast(FP8X4),
+                lhsT_scale=key_scales[:, rows],
+                rhs=note_words[:].bitcast(FP8X4),
+                rhs_scale=note_scales[:],
+                start=True,
+                stop=True,
+            )
+
+        factors = [keep.tile([P, J], F32, name="factors%d" % r) for r in range(TILES)]
+        table = [keep.tile([P, J], F32, name="table%d" % r) for r in range(TILES)]
+
+        def pick_given_s(r, a, b):
+            nc.scalar.activation(factors[r][:, a:b], given_rows[r][:].indirect(entries(given_list, a, b)), COPY)
+
+        def multiply(r):
+            nc.vector.tensor_tensor(table[r][:], sums[r][:], factors[r][:], MULT)
+
+        def place_v(r, a, b):
+            nc.vector.tensor_copy(placed[r][:].indirect(entries(place_list, a, b)), table[r][:, a:b])
+
+        def place_s(r, a, b):
+            nc.scalar.activation(placed[r][:].indirect(entries(place_list, a, b)), table[r][:, a:b], COPY)
+
+        def finish(r, a, b):
+            nc.vector.scalar_tensor_tensor(
+                result[r][:, a:b], old_rows[r][:, a:b], fade_cols[:, r : r + 1], placed[r][:, a:b], MULT, ADD
+            )
+            nc.sync.dma_start(out[r * P : (r + 1) * P, a:b], result[r][:, a:b])
+
+        for r in range(TILES - 1):
+            pick_given_s(r, 0, J)
+            multiply(r)
+        pick_given_s(3, 0, J)
+        place_v(0, 0, J)
+        multiply(3)
+        place_v(3, 0, SHARE)
+        for r in (1, 2):
+            place_s(r, 0, HALF)
+            place_s(r, HALF, J)
+        place_s(3, SHARE, J)
+        for r in range(TILES - 1):
+            finish(r, 0, M)
+        finish(3, 0, M // 2)
+        finish(3, M // 2, M)

@@ -19,7 +19,8 @@ PACK = 4
 D, T, I, J, U, Z, M = 512, 2048, 512, 512, 1024, 1024, 1024
 TILES = I // P
 HALF = J // 2
-SHARE = 320
+EARLY = 320
+WEAVE = 320
 FLOPS = 2 * D * I * J
 
 
@@ -47,13 +48,13 @@ def tile_attend_tab_timestable_keep_kernel(
         given_rows = [keep.tile([P, Z], F32, name="given_rows%d" % r) for r in range(TILES)]
         old_rows = [keep.tile([P, M], F32, name="old_rows%d" % r) for r in range(TILES)]
         placed = [keep.tile([P, M], F32, name="placed%d" % r) for r in range(TILES)]
+        fade_cols = keep.tile([P, TILES], F32, name="fade_cols")
         result = [keep.tile([P, M], F32, name="result%d" % r) for r in range(TILES)]
         fade_rows = keep.tile([P, P], F32, name="fade_rows")
         identity = keep.tile([P, P], F32, name="identity")
-        fade_cols = keep.tile([P, TILES], F32, name="fade_cols")
 
-        nc.gpsimd.memset(fade_rows[:], 0.0)
         nc.gpsimd.memset(pool_scales[:].bitcast(I32), 0)
+        nc.gpsimd.memset(fade_rows[:], 0.0)
         make_identity(nc, identity[:])
         for r in range(TILES):
             (nc.vector if r < 2 else nc.gpsimd).memset(placed[r][:], 0.0)
@@ -61,45 +62,48 @@ def tile_attend_tab_timestable_keep_kernel(
         notes_by_place = notes.rearrange("(p t) u -> t p u", t=PACK)
         scale_rows = keys_scales[0].bitcast(I32)
         nc.sync.dma_start(note_list[:], offs2)
-        nc.sync.dma_start(fade_rows[0:TILES, :], fade.rearrange("(r p) o -> r (p o)", p=P))
         nc.sync.dma_start(note_rows[0][:], notes_by_place[0])
+        nc.sync.dma_start(key_list[:], offs)
         nc.sync.dma_start(note_rows[1][:], notes_by_place[1])
         for f in range(4):
             nc.sync.dma_start(pool_scales[f:P:32, :].bitcast(I32), scale_rows[f:16:4, :])
         nc.sync.dma_start(note_rows[2][:], notes_by_place[2])
         nc.sync.dma_start(note_rows[3][:], notes_by_place[3])
-        nc.sync.dma_start(key_list[:], offs)
+        nc.sync.dma_start(fade_rows[0:TILES, :], fade.rearrange("(r p) o -> r (p o)", p=P))
         nc.sync.dma_start(pool_words[:], keys_words[0].rearrange("p n t -> p (n t)").bitcast(I32))
         nc.sync.dma_start(given_list[:], offs3)
-        for r in range(TILES):
-            nc.sync.dma_start(given_rows[r][:], given[r * P : (r + 1) * P, :])
         nc.sync.dma_start(place_list[:], offs4)
         for r in range(TILES):
+            nc.sync.dma_start(given_rows[r][:], given[r * P : (r + 1) * P, :])
+        for r in (0, 1, 3, 2):
             nc.sync.dma_start(old_rows[r][:], old[r * P : (r + 1) * P, :])
 
-        turned = psum.tile([P, P], F32, name="turned")
-        nc.tensor.transpose(turned[:], fade_rows[:], identity[:])
-        nc.scalar.activation(fade_cols[:], turned[:, 0:TILES], COPY)
-
-        picked = keep.tile([P, PACK, J], BF16, name="picked")
+        picked = keep.tile([P, PACK, J], F32, name="picked")
         woven = keep.tile([P, J, PACK], BF16, name="woven", align_bytes=64)
         note_words = keep.tile([P, J], U32, name="note_words", align_bytes=64)
         note_scales = keep.tile([P, J], U8, name="note_scales", align_bytes=64)
         key_words = keep.tile([P, I], U32, name="key_words", align_bytes=64)
         key_scales = keep.tile([P, I], U8, name="key_scales", align_bytes=64)
 
-        for t in range(PACK - 1):
-            nc.scalar.activation(picked[:, t, :], note_rows[t][:].indirect(note_list[:]), COPY)
+        nc.scalar.activation(picked[:, 0, :], note_rows[0][:].indirect(note_list[:]), COPY)
+        nc.vector.tensor_copy(picked[:, 1, :], note_rows[1][:].indirect(note_list[:]))
+        nc.scalar.activation(picked[:, 2, :], note_rows[2][:].indirect(note_list[:]), COPY)
         nc.vector.tensor_copy(key_scales[:], pool_scales[:].indirect(key_list[:]))
-        nc.vector.tensor_copy(picked[:, 3, 0:HALF], note_rows[3][:].indirect(entries(note_list, 0, HALF)))
-        nc.scalar.activation(picked[:, 3, HALF:J], note_rows[3][:].indirect(entries(note_list, HALF, J)), COPY)
-        nc.vector.tensor_copy(woven[:], picked[:].rearrange("p t j -> p j t"))
-        nc.vector.tensor_copy(key_words[:], pool_words[:].bitcast(U32).indirect(key_list[:]))
+        nc.vector.tensor_copy(picked[:, 3, 0:WEAVE], note_rows[3][:].indirect(entries(note_list, 0, WEAVE)))
+        nc.scalar.activation(picked[:, 3, WEAVE:J], note_rows[3][:].indirect(entries(note_list, WEAVE, J)), COPY)
+        nc.vector.tensor_copy(woven[:, 0:WEAVE, :], picked[:, :, 0:WEAVE].rearrange("p t j -> p j t"))
+        nc.scalar.activation(woven[:, WEAVE:J, :], picked[:, :, WEAVE:J].rearrange("p t j -> p j t"), COPY)
         nc.vector.quantize_mx(
             out=note_words[:].bitcast(FP8X4),
             scales=note_scales[:],
             in_=woven[:].rearrange("p j t -> p (j t)"),
         )
+        for a, b in ((0, P), (P, I)):
+            nc.vector.tensor_copy(key_words[:, a:b], pool_words[:].bitcast(U32).indirect(entries(key_list, a, b)))
+
+        turned = psum.tile([P, P], F32, name="turned")
+        nc.tensor.transpose(turned[:], fade_rows[:], identity[:])
+        nc.scalar.activation(fade_cols[:], turned[:, 0:TILES], COPY)
 
         sums = [psum.tile([P, J], F32, name="sums%d" % r) for r in range(TILES)]
         for r in range(TILES):
@@ -115,19 +119,21 @@ def tile_attend_tab_timestable_keep_kernel(
             )
 
         factors = [keep.tile([P, J], F32, name="factors%d" % r) for r in range(TILES)]
-        table = [keep.tile([P, J], F32, name="table%d" % r) for r in range(TILES)]
+
+        def pick_given_v(r, a, b):
+            nc.vector.tensor_copy(factors[r][:, a:b], given_rows[r][:].indirect(entries(given_list, a, b)))
 
         def pick_given_s(r, a, b):
             nc.scalar.activation(factors[r][:, a:b], given_rows[r][:].indirect(entries(given_list, a, b)), COPY)
 
-        def multiply(r):
-            nc.vector.tensor_tensor(table[r][:], sums[r][:], factors[r][:], MULT)
+        def multiply(r, a, b, part):
+            nc.vector.tensor_tensor(part, sums[r][:, a:b], factors[r][:, a:b], MULT)
 
-        def place_v(r, a, b):
-            nc.vector.tensor_copy(placed[r][:].indirect(entries(place_list, a, b)), table[r][:, a:b])
+        def place_s(r, a, b, values):
+            nc.scalar.activation(placed[r][:].indirect(entries(place_list, a, b)), values, COPY)
 
-        def place_s(r, a, b):
-            nc.scalar.activation(placed[r][:].indirect(entries(place_list, a, b)), table[r][:, a:b], COPY)
+        def place_copy_v(r, a, b, values):
+            nc.vector.tensor_copy(placed[r][:].indirect(entries(place_list, a, b)), values)
 
         def finish(r, a, b):
             nc.vector.scalar_tensor_tensor(
@@ -135,18 +141,33 @@ def tile_attend_tab_timestable_keep_kernel(
             )
             nc.sync.dma_start(out[r * P : (r + 1) * P, a:b], result[r][:, a:b])
 
-        for r in range(TILES - 1):
+        pick_given_v(0, 0, HALF)
+        pick_given_s(0, HALF, J)
+        early = keep.tile([P, EARLY], F32, name="early")
+        multiply(0, 0, EARLY, early[:])
+        place_copy_v(0, 0, EARLY, early[:])
+        for r in range(1, TILES):
             pick_given_s(r, 0, J)
-            multiply(r)
-        pick_given_s(3, 0, J)
-        place_v(0, 0, J)
-        multiply(3)
-        place_v(3, 0, SHARE)
-        for r in (1, 2):
-            place_s(r, 0, HALF)
-            place_s(r, HALF, J)
-        place_s(3, SHARE, J)
-        for r in range(TILES - 1):
-            finish(r, 0, M)
+        middle = keep.tile([P, 2 * J - EARLY], F32, name="given_rows2")
+        multiply(1, 0, J, middle[:, 0:J])
+        multiply(0, EARLY, J, middle[:, J:])
+        place_copy_v(0, EARLY, J, middle[:, J:])
+        place_s(1, 0, HALF, middle[:, 0:HALF])
+        place_s(1, HALF, J, middle[:, HALF:J])
+        late = keep.tile([P, 2, J], F32, name="given_rows3")
+        multiply(3, 0, J, late[:, 0, :])
+        multiply(2, 0, J, late[:, 1, :])
+        place_copy_v(3, 0, J, late[:, 0, :])
+        place_s(2, 0, HALF, late[:, 1, 0:HALF])
+        place_s(2, HALF, J, late[:, 1, HALF:J])
+
+        faded = keep.tile([P, M], F32, name="faded")
+        nc.gpsimd.tensor_scalar(faded[:], old_rows[0][:], fade_cols[:, 0:1], 0.0, MULT, ADD)
+        nc.gpsimd.tensor_tensor(result[0][:], faded[:], placed[0][:], ADD)
+        nc.sync.dma_start(out[0:P, :], result[0][:])
+        finish(1, 0, M)
         finish(3, 0, M // 2)
         finish(3, M // 2, M)
+        finish(2, 0, M // 2)
+        finish(2, M // 2, 3 * M // 4)
+        finish(2, 3 * M // 4, M)

@@ -47,9 +47,10 @@ def tile_attend_tab_timestable_keep_kernel(
         note_rows = [keep.tile([P, U], F32, name="note_rows%d" % t) for t in range(PACK)]
         given_rows = [keep.tile([P, Z], F32, name="given_rows%d" % r) for r in range(TILES)]
         old_rows = [keep.tile([P, M], F32, name="old_rows%d" % r) for r in range(TILES)]
+        old_left = keep.tile([P, M // 2], F32, name="old_left")
         placed = [keep.tile([P, M], F32, name="placed%d" % r) for r in range(TILES)]
         fade_cols = keep.tile([P, TILES], F32, name="fade_cols")
-        result = [keep.tile([P, M], F32, name="result%d" % r) for r in range(TILES)]
+        result = {r: keep.tile([P, M], F32, name="result%d" % r) for r in range(1, TILES)}
         fade_rows = keep.tile([P, P], F32, name="fade_rows")
         identity = keep.tile([P, P], F32, name="identity")
 
@@ -75,7 +76,10 @@ def tile_attend_tab_timestable_keep_kernel(
         nc.sync.dma_start(place_list[:], offs4)
         for r in range(TILES):
             nc.sync.dma_start(given_rows[r][:], given[r * P : (r + 1) * P, :])
-        for r in (0, 1, 3, 2):
+        nc.sync.dma_start(old_rows[0][:], old[0:P, :])
+        nc.sync.dma_start(old_left[:], old[P : 2 * P, 0 : M // 2])
+        nc.sync.dma_start(old_rows[1][:, M // 2 : M], old[P : 2 * P, M // 2 : M])
+        for r in (3, 2):
             nc.sync.dma_start(old_rows[r][:], old[r * P : (r + 1) * P, :])
 
         picked = keep.tile([P, PACK, J], F32, name="picked")
@@ -162,10 +166,16 @@ def tile_attend_tab_timestable_keep_kernel(
         place_s(2, HALF, J, late[:, 1, HALF:J])
 
         faded = keep.tile([P, M], F32, name="faded")
+        faded_left = keep.tile([P, M // 2], F32, name="faded_left")
         nc.gpsimd.tensor_scalar(faded[:], old_rows[0][:], fade_cols[:, 0:1], 0.0, MULT, ADD)
+        nc.gpsimd.tensor_scalar(faded_left[:], old_left[:], fade_cols[:, 1:2], 0.0, MULT, ADD)
+        result[0] = keep.tile([P, M], F32, name="old_left")
         nc.gpsimd.tensor_tensor(result[0][:], faded[:], placed[0][:], ADD)
         nc.sync.dma_start(out[0:P, :], result[0][:])
-        finish(1, 0, M)
+        result_left = keep.tile([P, M // 2], F32, name="result_left")
+        nc.gpsimd.tensor_tensor(result_left[:], faded_left[:], placed[1][:, 0 : M // 2], ADD)
+        nc.sync.dma_start(out[P : 2 * P, 0 : M // 2], result_left[:])
+        finish(1, M // 2, M)
         finish(3, 0, M // 2)
         finish(3, M // 2, M)
         finish(2, 0, M // 2)

@@ -50,7 +50,6 @@ def tile_attend_tab_timestable_keep_kernel(
         old_left = keep.tile([P, M // 2], F32, name="old_left")
         placed = [keep.tile([P, M], F32, name="placed%d" % r) for r in range(TILES)]
         fade_cols = keep.tile([P, TILES], F32, name="fade_cols")
-        result = {r: keep.tile([P, M], F32, name="result%d" % r) for r in range(1, TILES)}
         fade_rows = keep.tile([P, P], F32, name="fade_rows")
         identity = keep.tile([P, P], F32, name="identity")
 
@@ -139,11 +138,11 @@ def tile_attend_tab_timestable_keep_kernel(
         def place_copy_v(r, a, b, values):
             nc.vector.tensor_copy(placed[r][:].indirect(entries(place_list, a, b)), values)
 
-        def finish(r, a, b):
+        def finish(r, a, b, sums_out):
             nc.vector.scalar_tensor_tensor(
-                result[r][:, a:b], old_rows[r][:, a:b], fade_cols[:, r : r + 1], placed[r][:, a:b], MULT, ADD
+                sums_out, old_rows[r][:, a:b], fade_cols[:, r : r + 1], placed[r][:, a:b], MULT, ADD
             )
-            nc.sync.dma_start(out[r * P : (r + 1) * P, a:b], result[r][:, a:b])
+            nc.sync.dma_start(out[r * P : (r + 1) * P, a:b], sums_out)
 
         pick_given_v(0, 0, HALF)
         pick_given_s(0, HALF, J)
@@ -169,15 +168,22 @@ def tile_attend_tab_timestable_keep_kernel(
         faded_left = keep.tile([P, M // 2], F32, name="faded_left")
         nc.gpsimd.tensor_scalar(faded[:], old_rows[0][:], fade_cols[:, 0:1], 0.0, MULT, ADD)
         nc.gpsimd.tensor_scalar(faded_left[:], old_left[:], fade_cols[:, 1:2], 0.0, MULT, ADD)
-        result[0] = keep.tile([P, M], F32, name="old_left")
-        nc.gpsimd.tensor_tensor(result[0][:], faded[:], placed[0][:], ADD)
-        nc.sync.dma_start(out[0:P, :], result[0][:])
+        result_first = keep.tile([P, M], F32, name="old_left")
+        nc.gpsimd.tensor_tensor(result_first[:], faded[:], placed[0][:], ADD)
+        nc.sync.dma_start(out[0:P, :], result_first[:])
         result_left = keep.tile([P, M // 2], F32, name="result_left")
         nc.gpsimd.tensor_tensor(result_left[:], faded_left[:], placed[1][:, 0 : M // 2], ADD)
         nc.sync.dma_start(out[P : 2 * P, 0 : M // 2], result_left[:])
-        finish(1, M // 2, M)
-        finish(3, 0, M // 2)
-        finish(3, M // 2, M)
-        finish(2, 0, M // 2)
-        finish(2, M // 2, 3 * M // 4)
-        finish(2, 3 * M // 4, M)
+        pieces = (
+            (1, M // 2, M),
+            (3, 0, M // 2),
+            (3, M // 2, M),
+            (2, 0, M // 2),
+            (2, M // 2, 3 * M // 4),
+            (2, 3 * M // 4, M),
+        )
+        result_rest = keep.tile([P, 5 * M // 2], F32, name="faded")
+        at = 0
+        for r, a, b in pieces:
+            finish(r, a, b, result_rest[:, at : at + b - a])
+            at = at + b - a

from contextlib import ExitStack

import concourse.mybir as mybir
from concourse.masks import make_identity

F32 = mybir.dt.float32
BF16 = mybir.dt.bfloat16
I32 = mybir.dt.int32
U32 = mybir.dt.uint32
U16 = mybir.dt.uint16
U8 = mybir.dt.uint8
FP8X4 = mybir.dt.float8_e4m3fn_x4
MULT = mybir.AluOpType.mult
ADD = mybir.AluOpType.add
COPY = mybir.ActivationFunctionType.Copy

P = 128
PACK = 4
D, T, I, J, U, Z, M = 512, 2048, 512, 512, 1024, 1024, 1024
TILES = I // P
HALF = J // 2
EARLY = 320
WEAVE = 320
FLOPS = 2 * D * I * J


def tile_attend_tab_timestable_keep_kernel(
    tc, keys_words, keys_scales, notes, given, old, fade, offs, offs2, offs3, offs4, out
):
    nc = tc.nc

    def entries(listed, first, last):
        return listed[:, first // 16 : last // 16]

    with ExitStack() as ctx:
        lists = ctx.enter_context(tc.tile_pool(name="lists", bufs=1))
        keep = ctx.enter_context(tc.tile_pool(name="keep", bufs=1))
        psum = ctx.enter_context(tc.psum_pool(name="psum", bufs=1))

        key_list = lists.tile([P, I // 16], U16, name="key_list")
        note_list = lists.tile([P, J // 16], U16, name="note_list")
        given_list = lists.tile([P, J // 16], U16, name="given_list")
        place_list = lists.tile([P, J // 16], U16, name="place_list")

        pool_words = keep.tile([P, T], I32, name="pool_words", align_bytes=64)
        pool_scales = keep.tile([P, T], U8, name="pool_scales", align_bytes=64)
        note_rows = [keep.tile([P, U], F32, name="note_rows%d" % t) for t in range(PACK)]
        given_rows = [keep.tile([P, Z], F32, name="given_rows%d" % r) for r in range(TILES)]
        old_rows = [keep.tile([P, M], F32, name="old_rows%d" % r) for r in range(TILES)]
        old_left = keep.tile([P, M // 2], F32, name="old_left")
        placed = [keep.tile([P, M], F32, name="placed%d" % r) for r in range(TILES)]
        fade_cols = keep.tile([P, TILES], F32, name="fade_cols")
        fade_rows = keep.tile([P, P], F32, name="fade_rows")
        identity = keep.tile([P, P], F32, name="identity")

        nc.gpsimd.memset(pool_scales[:].bitcast(I32), 0)
        nc.gpsimd.memset(fade_rows[:], 0.0)
        make_identity(nc, identity[:])
        for r in range(TILES):
            (nc.vector if r < 2 else nc.gpsimd).memset(placed[r][:], 0.0)

        notes_by_place = notes.rearrange("(p t) u -> t p u", t=PACK)
        scale_rows = keys_scales[0].bitcast(I32)
        nc.sync.dma_start(note_list[:], offs2)
        nc.sync.dma_start(note_rows[0][:], notes_by_place[0])
        nc.sync.dma_start(key_list[:], offs)
        nc.sync.dma_start(note_rows[1][:], notes_by_place[1])
        for f in range(4):
            nc.sync.dma_start(pool_scales[f:P:32, :].bitcast(I32), scale_rows[f:16:4, :])
        nc.sync.dma_start(note_rows[2][:], notes_by_place[2])
        nc.sync.dma_start(note_rows[3][:], notes_by_place[3])
        nc.sync.dma_start(fade_rows[0:TILES, :], fade.rearrange("(r p) o -> r (p o)", p=P))
        nc.sync.dma_start(pool_words[:], keys_words[0].rearrange("p n t -> p (n t)").bitcast(I32))
        nc.sync.dma_start(given_list[:], offs3)
        nc.sync.dma_start(place_list[:], offs4)
        for r in range(TILES):
            nc.sync.dma_start(given_rows[r][:], given[r * P : (r + 1) * P, :])
        nc.sync.dma_start(old_rows[0][:], old[0:P, :])
        nc.sync.dma_start(old_left[:], old[P : 2 * P, 0 : M // 2])
        nc.sync.dma_start(old_rows[1][:, M // 2 : M], old[P : 2 * P, M // 2 : M])
        for r in (3, 2):
            nc.sync.dma_start(old_rows[r][:], old[r * P : (r + 1) * P, :])

        picked = keep.tile([P, PACK, J], F32, name="picked")
        woven = keep.tile([P, J, PACK], BF16, name="woven", align_bytes=64)
        note_words = keep.tile([P, J], U32, name="note_words", align_bytes=64)
        note_scales = keep.tile([P, J], U8, name="note_scales", align_bytes=64)
        key_words = keep.tile([P, I], U32, name="key_words", align_bytes=64)
        key_scales = keep.tile([P, I], U8, name="key_scales", align_bytes=64)

        nc.scalar.activation(picked[:, 0, :], note_rows[0][:].indirect(note_list[:]), COPY)
        nc.vector.tensor_copy(picked[:, 1, :], note_rows[1][:].indirect(note_list[:]))
        nc.scalar.activation(picked[:, 2, :], note_rows[2][:].indirect(note_list[:]), COPY)
        nc.vector.tensor_copy(key_scales[:], pool_scales[:].indirect(key_list[:]))
        nc.vector.tensor_copy(picked[:, 3, 0:WEAVE], note_rows[3][:].indirect(entries(note_list, 0, WEAVE)))
        nc.scalar.activation(picked[:, 3, WEAVE:J], note_rows[3][:].indirect(entries(note_list, WEAVE, J)), COPY)
        nc.vector.tensor_copy(woven[:, 0:WEAVE, :], picked[:, :, 0:WEAVE].rearrange("p t j -> p j t"))
        nc.scalar.activation(woven[:, WEAVE:J, :], picked[:, :, WEAVE:J].rearrange("p t j -> p j t"), COPY)
        nc.vector.quantize_mx(
            out=note_words[:].bitcast(FP8X4),
            scales=note_scales[:],
            in_=woven[:].rearrange("p j t -> p (j t)"),
        )
        for a, b in ((0, P), (P, I)):
            nc.vector.tensor_copy(key_words[:, a:b], pool_words[:].bitcast(U32).indirect(entries(key_list, a, b)))

        turned = psum.tile([P, P], F32, name="turned")
        nc.tensor.transpose(turned[:], fade_rows[:], identity[:])
        nc.scalar.activation(fade_cols[:], turned[:, 0:TILES], COPY)

        sums = [psum.tile([P, J], F32, name="sums%d" % r) for r in range(TILES)]
        for r in range(TILES):
            rows = slice(r * P, (r + 1) * P)
            nc.tensor.matmul_mx(
                out=sums[r][:],
                lhsT=key_words[:, rows].bitcast(FP8X4),
                lhsT_scale=key_scales[:, rows],
                rhs=note_words[:].bitcast(FP8X4),
                rhs_scale=note_scales[:],
                start=True,
                stop=True,
            )

        factors = [keep.tile([P, J], F32, name="factors%d" % r) for r in range(TILES)]

        def pick_given_v(r, a, b):
            nc.vector.tensor_copy(factors[r][:, a:b], given_rows[r][:].indirect(entries(given_list, a, b)))

        def pick_given_s(r, a, b):
            nc.scalar.activation(factors[r][:, a:b], given_rows[r][:].indirect(entries(given_list, a, b)), COPY)

        def multiply(r, a, b, part):
            nc.vector.tensor_tensor(part, sums[r][:, a:b], factors[r][:, a:b], MULT)

        def place_s(r, a, b, values):
            nc.scalar.activation(placed[r][:].indirect(entries(place_list, a, b)), values, COPY)

        def place_copy_v(r, a, b, values):
            nc.vector.tensor_copy(placed[r][:].indirect(entries(place_list, a, b)), values)

        def finish(r, a, b, sums_out):
            nc.vector.scalar_tensor_tensor(
                sums_out, old_rows[r][:, a:b], fade_cols[:, r : r + 1], placed[r][:, a:b], MULT, ADD
            )
            nc.sync.dma_start(out[r * P : (r + 1) * P, a:b], sums_out)

        pick_given_v(0, 0, HALF)
        pick_given_s(0, HALF, J)
        early = keep.tile([P, EARLY], F32, name="early")
        multiply(0, 0, EARLY, early[:])
        place_copy_v(0, 0, EARLY, early[:])
        for r in range(1, TILES):
            pick_given_s(r, 0, J)
        middle = keep.tile([P, 2 * J - EARLY], F32, name="given_rows2")
        multiply(1, 0, J, middle[:, 0:J])
        multiply(0, EARLY, J, middle[:, J:])
        place_copy_v(0, EARLY, J, middle[:, J:])
        place_s(1, 0, HALF, middle[:, 0:HALF])
        place_s(1, HALF, J, middle[:, HALF:J])
        late = keep.tile([P, 2, J], F32, name="given_rows3")
        multiply(3, 0, J, late[:, 0, :])
        multiply(2, 0, J, late[:, 1, :])
        place_copy_v(3, 0, J, late[:, 0, :])
        place_s(2, 0, HALF, late[:, 1, 0:HALF])
        place_s(2, HALF, J, late[:, 1, HALF:J])

        faded = keep.tile([P, M], F32, name="faded")
        faded_left = keep.tile([P, M // 2], F32, name="faded_left")
        nc.gpsimd.tensor_scalar(faded[:], old_rows[0][:], fade_cols[:, 0:1], 0.0, MULT, ADD)
        nc.gpsimd.tensor_scalar(faded_left[:], old_left[:], fade_cols[:, 1:2], 0.0, MULT, ADD)
        result_first = keep.tile([P, M], F32, name="old_left")
        nc.gpsimd.tensor_tensor(result_first[:], faded[:], placed[0][:], ADD)
        nc.sync.dma_start(out[0:P, :], result_first[:])
        result_left = keep.tile([P, M // 2], F32, name="result_left")
        nc.gpsimd.tensor_tensor(result_left[:], faded_left[:], placed[1][:, 0 : M // 2], ADD)
        nc.sync.dma_start(out[P : 2 * P, 0 : M // 2], result_left[:])
        pieces = (
            (1, M // 2, M),
            (3, 0, M // 2),
            (3, M // 2, M),
            (2, 0, M // 2),
            (2, M // 2, 3 * M // 4),
            (2, 3 * M // 4, M),
        )
        result_rest = keep.tile([P, 5 * M // 2], F32, name="faded")
        at = 0
        for r, a, b in pieces:
            finish(r, a, b, result_rest[:, at : at + b - a])
            at = at + b - a
